import numpy as np
import ml_dtypes


def mxq(x, axis, fmt="e4m3"):
    dtype, down = {"e4m3": (ml_dtypes.float8_e4m3fn, 7), "e5m2": (ml_dtypes.float8_e5m2, 14)}[fmt]
    v = np.moveaxis(np.asarray(x, np.float32).astype(ml_dtypes.bfloat16).astype(np.float64), axis, -1)
    blocks = v.reshape(v.shape[:-1] + (-1, 32))
    amax = np.abs(blocks).max(-1, keepdims=True)
    byte = np.maximum(np.where(amax > 0, np.frexp(amax)[1] - 1 + 127, 0) - down, 1)
    scale = np.exp2(byte - 127.0)
    codes = (blocks / scale).astype(np.float32).astype(dtype).astype(np.float64)
    return np.moveaxis((codes * scale).reshape(v.shape), -1, axis)


WIDE = False


def mx_kscale(k):
    if not WIDE:
        return np.ones(k)
    levels = np.array([10, -10, 5, -5, 0])
    if k % 512:
        return np.exp2(np.random.permutation(np.resize(levels, k // 32))).repeat(32)
    a = np.empty((k // 512, 16))
    for p in range(k // 512):
        a[p, :8] = np.random.permutation(np.resize(levels, 8))
        for g in range(8):
            far = levels[np.abs(levels - a[p, g]) >= 10]
            a[p, g + 8] = far[np.random.randint(len(far))]
    return np.exp2(a.ravel()).repeat(32)


def f64(x):
    return np.asarray(x).astype(np.float64)


def striped8(idx):
    return np.asarray(idx).reshape(8, -1, 16).transpose(0, 2, 1).reshape(128, -1).astype(np.uint16)


def unstriped8(offs):
    return offs.reshape(8, 16, -1).transpose(0, 2, 1).reshape(8, -1).astype(np.int64)


def pick8(x, idx, run):
    r = np.arange(len(x))
    return x[r[:, None], idx[r % (8 * run) // run]]


E2M1 = np.array([0.0, 0.5, 1.0, 1.5, 2.0, 3.0, 4.0, 6.0, -0.0, -0.5, -1.0, -1.5, -2.0, -3.0, -4.0, -6.0])


def pack_weight(w, fmt):
    k, n = w.shape
    w = f64(np.asarray(w, np.float32).astype(ml_dtypes.bfloat16)).reshape(k // 32, 32, n)
    amax = np.abs(w).max(1)
    if fmt == "e4m3":
        byte = np.frexp(amax)[1] - 1 + 127 - 7
    else:
        mant, ex = np.frexp(amax / 6.0)
        byte = np.where(mant > 0.5, ex, ex - 1) + 127
    byte = np.clip(np.where(amax > 0, byte, 1), 1, 254)
    scaled = (w * np.exp2(127.0 - byte)[:, None, :]).reshape(k, n).astype(np.float32)
    by_word = np.ascontiguousarray(scaled.reshape(k // 512, 128, 4, n).transpose(0, 1, 3, 2))
    if fmt == "e4m3":
        words = by_word.astype(ml_dtypes.float8_e4m3fn).view(np.uint8)
    else:
        c = by_word.astype(ml_dtypes.float4_e2m1fn).view(np.uint8) & 0xF
        words = (c[..., 0::2] | (c[..., 1::2] << 4)).reshape(k // 512, 128, 2 * n)
    return np.ascontiguousarray(words), np.ascontiguousarray(byte.astype(np.uint8).reshape(k // 512, 16, n))


def unpack_weight(words, scales, fmt):
    g, _, n = scales.shape
    words = np.ascontiguousarray(words).reshape(g, 128, n, -1)
    if fmt == "e4m3":
        vals = words.view(ml_dtypes.float8_e4m3fn).astype(np.float64)
    else:
        nib = np.empty((g, 128, n, 4), np.uint8)
        nib[..., 0::2] = words & 0xF
        nib[..., 1::2] = words >> 4
        vals = E2M1[nib]
    vals = vals * np.repeat(np.exp2(scales.astype(np.float64) - 127.0), 8, axis=1)[..., None]
    return vals.transpose(0, 1, 3, 2).reshape(g * 512, n)


D, T, I, Q = 512, 1024, 512, 128


def setup_inputs():
    n = np.random.standard_normal
    idx = np.stack([np.random.permutation(T)[:I] for _ in range(8)])
    idx2 = np.stack([np.random.permutation(T)[:I] for _ in range(8)])
    idx3 = np.stack([np.random.permutation(T)[:I] for _ in range(8)])
    idx4 = np.stack([np.random.permutation(T)[:I] for _ in range(8)])
    fd = mx_kscale(D)
    keysp = pack_weight(n((D, T)) / fd[:, None], "e2m1")
    return {
        "query": (n((D, Q)) * 1.0 / np.sqrt(D) * fd[:, None]).astype(np.float32),
        "keys_words": keysp[0],
        "keys_scales": keysp[1],
        "old": (np.random.uniform(0.3, 1.7, (Q, T))).astype(np.float32),
        "base": (0.5 * n((Q, T))).astype(np.float32),
        "offs": striped8(idx),
        "offs2": striped8(idx2),
        "offs3": striped8(idx3),
        "offs4": striped8(idx4),
    }


def reference(query, keys_words, keys_scales, old, base, offs, offs2, offs3, offs4):
    idx = unstriped8(offs)
    idx2 = unstriped8(offs2)
    idx3 = unstriped8(offs3)
    idx4 = unstriped8(offs4)
    keysu = unpack_weight(keys_words, keys_scales, "e2m1")
    queryq = mxq(f64(query), 0, "e4m3")
    a = queryq.T @ keysu
    s = pick8(a, idx, 16) * pick8(a, idx2, 16)
    p = np.exp(s - np.max(s, axis=1, keepdims=True))
    w = p / np.sum(p, axis=1, keepdims=True)
    ws = w * pick8(f64(old), idx3, 16) * 256.0
    f1 = np.zeros((Q, T))
    f1[np.arange(Q)[:, None], idx4[np.arange(Q) % 128 // 16]] = ws
    y = f64(base) + f1
    return y

@@ -1,0 +1,142 @@
+from contextlib import ExitStack
+
+import concourse.mybir as mybir
+
+D, T, SLOTS, Q = 512, 1024, 512, 128
+FLOPS = 2 * D * Q * T
+
+F32 = mybir.dt.float32
+BF16 = mybir.dt.bfloat16
+I32 = mybir.dt.int32
+U32 = mybir.dt.uint32
+U16 = mybir.dt.uint16
+U8 = mybir.dt.uint8
+FP8X4 = mybir.dt.float8_e4m3fn_x4
+FP4X4 = mybir.dt.float4_e2m1fn_x4
+ALU = mybir.AluOpType
+ACT = mybir.ActivationFunctionType
+
+P = 128
+PACK = 4
+PER_COL = 16
+HALF = SLOTS // 2
+TOKEN_CHUNKS = (256, 256, 256, 128, 128)
+FIRST_SCATTER = 128
+OUT_CHUNK = 256
+
+
+def tile_attend_pairproduct_soft_timesold_heads_kernel(
+    tc, query, keys_words, keys_scales, old, base, offs, offs2, offs3, offs4, out
+):
+    nc = tc.nc
+    with ExitStack() as ctx:
+        keep = ctx.enter_context(tc.tile_pool(name="keep", bufs=1))
+        psum = ctx.enter_context(tc.psum_pool(name="psum", bufs=1))
+
+        def slots(list_tile, lo, hi):
+            return list_tile[:, lo // PER_COL : hi // PER_COL]
+
+        q_raw = keep.tile([P, PACK, Q], F32, name="q_raw")
+        nc.sync.dma_start(out=q_raw[:], in_=query.rearrange("(p j) q -> p j q", j=PACK))
+        k_words = keep.tile([P, 2 * T], U8, name="k_words", align_bytes=64)
+        nc.sync.dma_start(out=k_words[:].bitcast(I32), in_=keys_words[0].bitcast(I32))
+
+        k_scales = keep.tile([P, T], U8, name="k_scales", align_bytes=64)
+        nc.vector.memset(k_scales[:].bitcast(U32), 0)
+        for quad in range(4):
+            nc.scalar.dma_start(
+                out=k_scales[32 * quad : 32 * quad + 4, :].bitcast(I32),
+                in_=keys_scales[0, 4 * quad : 4 * quad + 4, :].bitcast(I32),
+            )
+
+        lists = []
+        for name, src in (("idx", offs), ("idx2", offs2), ("idx3", offs3), ("idx4", offs4)):
+            lists.append(keep.tile([P, SLOTS // PER_COL], U16, name=name))
+        idx, idx2, idx3, idx4 = lists
+        old_sb = keep.tile([P, T], F32, name="old_sb")
+        base_sb = keep.tile([P, T], F32, name="base_sb")
+        nc.sync.dma_start(idx[:], offs)
+        nc.sync.dma_start(idx2[:], offs2)
+        nc.sync.dma_start(idx3[:], offs3)
+        nc.sync.dma_start(out=old_sb[:], in_=old)
+        nc.sync.dma_start(idx4[:], offs4)
+        nc.sync.dma_start(out=base_sb[:], in_=base)
+
+        placed = keep.tile([P, T], F32, name="placed")
+        nc.vector.memset(placed[:], 0.0)
+
+        q_bf = keep.tile([P, Q, PACK], BF16, name="q_bf", align_bytes=64)
+        q_codes = keep.tile([P, Q], U32, name="q_codes", align_bytes=64)
+        q_scales = keep.tile([P, Q], U8, name="q_scales", align_bytes=64)
+        qh = Q // 2
+        q_view = q_raw[:].rearrange("p j q -> p q j")
+        nc.scalar.activation(q_bf[:, 0:qh, :], q_view[:, 0:qh, :], ACT.Copy)
+        nc.vector.tensor_copy(out=q_bf[:, qh:Q, :], in_=q_view[:, qh:Q, :])
+        for lo in (qh, 0):
+            nc.vector.quantize_mx(
+                out=q_codes[:, lo : lo + qh].bitcast(FP8X4),
+                scales=q_scales[:, lo : lo + qh],
+                in_=q_bf[:, lo : lo + qh, :].rearrange("p q j -> p (q j)"),
+            )
+
+        a = keep.tile([P, T], F32, name="a")
+        lo = 0
+        for c, width in enumerate(TOKEN_CHUNKS):
+            hi = lo + width
+            bank = psum.tile([P, width], F32, name="bank%d" % c)
+            nc.tensor.matmul_mx(
+                out=bank[:],
+                lhsT=q_codes[:].bitcast(FP8X4),
+                lhsT_scale=q_scales[:],
+                rhs=k_words[:, 2 * lo : 2 * hi].bitcast(FP4X4),
+                rhs_scale=k_scales[:, lo:hi],
+                start=True,
+                stop=True,
+            )
+            if c % 2 == 0:
+                nc.vector.tensor_copy(out=a[:, lo:hi], in_=bank[:])
+            else:
+                nc.scalar.copy(a[:, lo:hi], bank[:])
+            lo = hi
+
+        left = keep.tile([P, SLOTS], F32, name="left")
+        right = keep.tile([P, HALF], F32, name="right", tag="reused")
+        s = keep.tile([P, SLOTS], F32, name="s")
+        neg_s = keep.tile([P, SLOTS], F32, name="neg_s")
+        neg_max_first = keep.tile([P, 1], F32, name="neg_max_first")
+        neg_max = keep.tile([P, 1], F32, name="neg_max")
+        nc.scalar.activation(left[:, 0:HALF], a[:].indirect(slots(idx, 0, HALF)), ACT.Copy)
+        nc.scalar.activation(left[:, HALF:SLOTS], a[:].indirect(slots(idx, HALF, SLOTS)), ACT.Copy)
+        nc.vector.tensor_copy(right[:], a[:].indirect(slots(idx2, 0, HALF)))
+        nc.vector.tensor_tensor(s[:, 0:HALF], left[:, 0:HALF], right[:], ALU.mult)
+        nc.vector.tensor_scalar(
+            neg_s[:, 0:HALF], s[:, 0:HALF], -1.0, None, ALU.mult, ALU.min, accum_out=neg_max_first[:]
+        )
+        nc.vector.tensor_tensor(
+            s[:, HALF:SLOTS], a[:].indirect(slots(idx2, HALF, SLOTS)), left[:, HALF:SLOTS], ALU.mult
+        )
+        nc.vector.tensor_scalar(
+            neg_s[:, HALF:SLOTS], s[:, HALF:SLOTS], -1.0, neg_max_first[:], ALU.mult, ALU.min, accum_out=neg_max[:]
+        )
+
+        old_listed = keep.tile([P, SLOTS], F32, name="old_listed", tag="reused")
+        nc.scalar.activation(old_listed[:], old_sb[:].indirect(idx3[:]), ACT.Copy, scale=256.0)
+
+        p = keep.tile([P, SLOTS], F32, name="p")
+        row_sum = keep.tile([P, 1], F32, name="row_sum")
+        nc.scalar.activation(p[:], neg_s[:], ACT.Exp, bias=neg_max[:], scale=-1.0, accum_out=row_sum[:])
+        inv_sum = keep.tile([P, 1], F32, name="inv_sum")
+        nc.vector.reciprocal(inv_sum[:], row_sum[:])
+
+        factor = keep.tile([P, SLOTS], F32, name="factor")
+        cut = FIRST_SCATTER
+        nc.vector.tensor_scalar(factor[:, 0:cut], old_listed[:, 0:cut], inv_sum[:], None, ALU.mult)
+        nc.scalar.activation(factor[:, cut:SLOTS], old_listed[:, cut:SLOTS], ACT.Copy, scale=inv_sum[:])
+        for lo, hi in ((0, cut), (cut, SLOTS)):
+            nc.vector.tensor_tensor(placed[:].indirect(slots(idx4, lo, hi)), p[:, lo:hi], factor[:, lo:hi], ALU.mult)
+
+        result = keep.tile([P, T], F32, name="result")
+        for lo in range(0, T, OUT_CHUNK):
+            cols = slice(lo, lo + OUT_CHUNK)
+            nc.vector.tensor_tensor(result[:, cols], placed[:, cols], base_sb[:, cols], ALU.add)
+            nc.sync.dma_start(out=out[:, cols], in_=result[:, cols])

@@ -15,14 +15,14 @@ FP8X4 = mybir.dt.float8_e4m3fn_x4
 FP4X4 = mybir.dt.float4_e2m1fn_x4
 ALU = mybir.AluOpType
 ACT = mybir.ActivationFunctionType
+AXIS_X = mybir.AxisListType.X
 
 P = 128
 PACK = 4
 PER_COL = 16
 HALF = SLOTS // 2
 TOKEN_CHUNKS = (256, 256, 256, 128, 128)
-FIRST_SCATTER = 128
-OUT_CHUNK = 256
+OUT_CHUNKS = (128, 384, 384, 128)
 
 
 def tile_attend_pairproduct_soft_timesold_heads_kernel(
@@ -44,7 +44,7 @@ def tile_attend_pairproduct_soft_timesold_heads_kernel(
         k_scales = keep.tile([P, T], U8, name="k_scales", align_bytes=64)
         nc.vector.memset(k_scales[:].bitcast(U32), 0)
         for quad in range(4):
-            nc.scalar.dma_start(
+            nc.sync.dma_start(
                 out=k_scales[32 * quad : 32 * quad + 4, :].bitcast(I32),
                 in_=keys_scales[0, 4 * quad : 4 * quad + 4, :].bitcast(I32),
             )
@@ -100,43 +100,41 @@ def tile_attend_pairproduct_soft_timesold_heads_kernel(
             lo = hi
 
         left = keep.tile([P, SLOTS], F32, name="left")
-        right = keep.tile([P, HALF], F32, name="right", tag="reused")
-        s = keep.tile([P, SLOTS], F32, name="s")
-        neg_s = keep.tile([P, SLOTS], F32, name="neg_s")
-        neg_max_first = keep.tile([P, 1], F32, name="neg_max_first")
+        right = keep.tile([P, SLOTS], F32, name="right", tag="reused")
+        s = keep.tile([P, SLOTS + 1], F32, name="s")
+        halves = ((0, HALF), (HALF, SLOTS))
+        for lo, hi in halves:
+            nc.scalar.activation(left[:, lo:hi], a[:].indirect(slots(idx, lo, hi)), ACT.Copy)
+            nc.vector.tensor_copy(right[:, lo:hi], a[:].indirect(slots(idx2, lo, hi)))
         neg_max = keep.tile([P, 1], F32, name="neg_max")
-        nc.scalar.activation(left[:, 0:HALF], a[:].indirect(slots(idx, 0, HALF)), ACT.Copy)
-        nc.scalar.activation(left[:, HALF:SLOTS], a[:].indirect(slots(idx, HALF, SLOTS)), ACT.Copy)
-        nc.vector.tensor_copy(right[:], a[:].indirect(slots(idx2, 0, HALF)))
-        nc.vector.tensor_tensor(s[:, 0:HALF], left[:, 0:HALF], right[:], ALU.mult)
-        nc.vector.tensor_scalar(
-            neg_s[:, 0:HALF], s[:, 0:HALF], -1.0, None, ALU.mult, ALU.min, accum_out=neg_max_first[:]
-        )
-        nc.vector.tensor_tensor(
-            s[:, HALF:SLOTS], a[:].indirect(slots(idx2, HALF, SLOTS)), left[:, HALF:SLOTS], ALU.mult
-        )
-        nc.vector.tensor_scalar(
-            neg_s[:, HALF:SLOTS], s[:, HALF:SLOTS], -1.0, neg_max_first[:], ALU.mult, ALU.min, accum_out=neg_max[:]
-        )
+        nc.vector.tensor_tensor(s[:, 0:HALF], left[:, 0:HALF], right[:, 0:HALF], ALU.mult)
+        nc.vector.tensor_reduce(s[:, SLOTS : SLOTS + 1], s[:, 0:HALF], AXIS_X, ALU.max)
+        nc.vector.tensor_tensor(s[:, HALF:SLOTS], left[:, HALF:SLOTS], right[:, HALF:SLOTS], ALU.mult)
+        nc.vector.tensor_reduce(neg_max[:], s[:, HALF : SLOTS + 1], AXIS_X, ALU.max, negate=True)
 
         old_listed = keep.tile([P, SLOTS], F32, name="old_listed", tag="reused")
-        nc.scalar.activation(old_listed[:], old_sb[:].indirect(idx3[:]), ACT.Copy, scale=256.0)
+        nc.scalar.activation(
+            old_listed[:, HALF:SLOTS], old_sb[:].indirect(slots(idx3, HALF, SLOTS)), ACT.Copy, scale=256.0
+        )
+        nc.vector.tensor_scalar(
+            old_listed[:, 0:HALF], old_sb[:].indirect(slots(idx3, 0, HALF)), 256.0, 0.0, ALU.mult, ALU.add
+        )
 
         p = keep.tile([P, SLOTS], F32, name="p")
         row_sum = keep.tile([P, 1], F32, name="row_sum")
-        nc.scalar.activation(p[:], neg_s[:], ACT.Exp, bias=neg_max[:], scale=-1.0, accum_out=row_sum[:])
+        nc.scalar.activation(p[:], s[:, 0:SLOTS], ACT.Exp, bias=neg_max[:], accum_out=row_sum[:])
         inv_sum = keep.tile([P, 1], F32, name="inv_sum")
         nc.vector.reciprocal(inv_sum[:], row_sum[:])
 
         factor = keep.tile([P, SLOTS], F32, name="factor")
-        cut = FIRST_SCATTER
-        nc.vector.tensor_scalar(factor[:, 0:cut], old_listed[:, 0:cut], inv_sum[:], None, ALU.mult)
-        nc.scalar.activation(factor[:, cut:SLOTS], old_listed[:, cut:SLOTS], ACT.Copy, scale=inv_sum[:])
-        for lo, hi in ((0, cut), (cut, SLOTS)):
-            nc.vector.tensor_tensor(placed[:].indirect(slots(idx4, lo, hi)), p[:, lo:hi], factor[:, lo:hi], ALU.mult)
+        nc.vector.tensor_scalar(factor[:], old_listed[:], inv_sum[:], None, ALU.mult)
+        nc.vector.tensor_tensor(placed[:].indirect(idx4[:]), p[:], factor[:], ALU.mult)
 
         result = keep.tile([P, T], F32, name="result")
-        for lo in range(0, T, OUT_CHUNK):
-            cols = slice(lo, lo + OUT_CHUNK)
+        lo = 0
+        for c, width in enumerate(OUT_CHUNKS):
+            cols = slice(lo, lo + width)
             nc.vector.tensor_tensor(result[:, cols], placed[:, cols], base_sb[:, cols], ALU.add)
-            nc.sync.dma_start(out=out[:, cols], in_=result[:, cols])
+            queue = nc.sync if c % 2 == 0 else nc.scalar
+            queue.dma_start(out=out[:, cols], in_=result[:, cols])
+            lo = lo + width

from contextlib import ExitStack

import concourse.mybir as mybir

D, T, SLOTS, Q = 512, 1024, 512, 128
FLOPS = 2 * D * Q * T

F32 = mybir.dt.float32
BF16 = mybir.dt.bfloat16
I32 = mybir.dt.int32
U32 = mybir.dt.uint32
U16 = mybir.dt.uint16
U8 = mybir.dt.uint8
FP8X4 = mybir.dt.float8_e4m3fn_x4
FP4X4 = mybir.dt.float4_e2m1fn_x4
ALU = mybir.AluOpType
ACT = mybir.ActivationFunctionType
AXIS_X = mybir.AxisListType.X

P = 128
PACK = 4
PER_COL = 16
HALF = SLOTS // 2
TOKEN_CHUNKS = (256, 256, 256, 128, 128)
OUT_CHUNKS = (128, 384, 384, 128)


def tile_attend_pairproduct_soft_timesold_heads_kernel(
    tc, query, keys_words, keys_scales, old, base, offs, offs2, offs3, offs4, out
):
    nc = tc.nc
    with ExitStack() as ctx:
        keep = ctx.enter_context(tc.tile_pool(name="keep", bufs=1))
        psum = ctx.enter_context(tc.psum_pool(name="psum", bufs=1))

        def slots(list_tile, lo, hi):
            return list_tile[:, lo // PER_COL : hi // PER_COL]

        q_raw = keep.tile([P, PACK, Q], F32, name="q_raw")
        nc.sync.dma_start(out=q_raw[:], in_=query.rearrange("(p j) q -> p j q", j=PACK))
        k_words = keep.tile([P, 2 * T], U8, name="k_words", align_bytes=64)
        nc.sync.dma_start(out=k_words[:].bitcast(I32), in_=keys_words[0].bitcast(I32))

        k_scales = keep.tile([P, T], U8, name="k_scales", align_bytes=64)
        nc.vector.memset(k_scales[:].bitcast(U32), 0)
        for quad in range(4):
            nc.sync.dma_start(
                out=k_scales[32 * quad : 32 * quad + 4, :].bitcast(I32),
                in_=keys_scales[0, 4 * quad : 4 * quad + 4, :].bitcast(I32),
            )

        lists = []
        for name, src in (("idx", offs), ("idx2", offs2), ("idx3", offs3), ("idx4", offs4)):
            lists.append(keep.tile([P, SLOTS // PER_COL], U16, name=name))
        idx, idx2, idx3, idx4 = lists
        old_sb = keep.tile([P, T], F32, name="old_sb")
        base_sb = keep.tile([P, T], F32, name="base_sb")
        nc.sync.dma_start(idx[:], offs)
        nc.sync.dma_start(idx2[:], offs2)
        nc.sync.dma_start(idx3[:], offs3)
        nc.sync.dma_start(out=old_sb[:], in_=old)
        nc.sync.dma_start(idx4[:], offs4)
        nc.sync.dma_start(out=base_sb[:], in_=base)

        placed = keep.tile([P, T], F32, name="placed")
        nc.vector.memset(placed[:], 0.0)

        q_bf = keep.tile([P, Q, PACK], BF16, name="q_bf", align_bytes=64)
        q_codes = keep.tile([P, Q], U32, name="q_codes", align_bytes=64)
        q_scales = keep.tile([P, Q], U8, name="q_scales", align_bytes=64)
        qh = Q // 2
        q_view = q_raw[:].rearrange("p j q -> p q j")
        nc.scalar.activation(q_bf[:, 0:qh, :], q_view[:, 0:qh, :], ACT.Copy)
        nc.vector.tensor_copy(out=q_bf[:, qh:Q, :], in_=q_view[:, qh:Q, :])
        for lo in (qh, 0):
            nc.vector.quantize_mx(
                out=q_codes[:, lo : lo + qh].bitcast(FP8X4),
                scales=q_scales[:, lo : lo + qh],
                in_=q_bf[:, lo : lo + qh, :].rearrange("p q j -> p (q j)"),
            )

        a = keep.tile([P, T], F32, name="a")
        lo = 0
        for c, width in enumerate(TOKEN_CHUNKS):
            hi = lo + width
            bank = psum.tile([P, width], F32, name="bank%d" % c)
            nc.tensor.matmul_mx(
                out=bank[:],
                lhsT=q_codes[:].bitcast(FP8X4),
                lhsT_scale=q_scales[:],
                rhs=k_words[:, 2 * lo : 2 * hi].bitcast(FP4X4),
                rhs_scale=k_scales[:, lo:hi],
                start=True,
                stop=True,
            )
            if c % 2 == 0:
                nc.vector.tensor_copy(out=a[:, lo:hi], in_=bank[:])
            else:
                nc.scalar.copy(a[:, lo:hi], bank[:])
            lo = hi

        left = keep.tile([P, SLOTS], F32, name="left")
        right = keep.tile([P, SLOTS], F32, name="right", tag="reused")
        s = keep.tile([P, SLOTS + 1], F32, name="s")
        halves = ((0, HALF), (HALF, SLOTS))
        for lo, hi in halves:
            nc.scalar.activation(left[:, lo:hi], a[:].indirect(slots(idx, lo, hi)), ACT.Copy)
            nc.vector.tensor_copy(right[:, lo:hi], a[:].indirect(slots(idx2, lo, hi)))
        neg_max = keep.tile([P, 1], F32, name="neg_max")
        nc.vector.tensor_tensor(s[:, 0:HALF], left[:, 0:HALF], right[:, 0:HALF], ALU.mult)
        nc.vector.tensor_reduce(s[:, SLOTS : SLOTS + 1], s[:, 0:HALF], AXIS_X, ALU.max)
        nc.vector.tensor_tensor(s[:, HALF:SLOTS], left[:, HALF:SLOTS], right[:, HALF:SLOTS], ALU.mult)
        nc.vector.tensor_reduce(neg_max[:], s[:, HALF : SLOTS + 1], AXIS_X, ALU.max, negate=True)

        old_listed = keep.tile([P, SLOTS], F32, name="old_listed", tag="reused")
        nc.scalar.activation(
            old_listed[:, HALF:SLOTS], old_sb[:].indirect(slots(idx3, HALF, SLOTS)), ACT.Copy, scale=256.0
        )
        nc.vector.tensor_scalar(
            old_listed[:, 0:HALF], old_sb[:].indirect(slots(idx3, 0, HALF)), 256.0, 0.0, ALU.mult, ALU.add
        )

        p = keep.tile([P, SLOTS], F32, name="p")
        row_sum = keep.tile([P, 1], F32, name="row_sum")
        nc.scalar.activation(p[:], s[:, 0:SLOTS], ACT.Exp, bias=neg_max[:], accum_out=row_sum[:])
        inv_sum = keep.tile([P, 1], F32, name="inv_sum")
        nc.vector.reciprocal(inv_sum[:], row_sum[:])

        factor = keep.tile([P, SLOTS], F32, name="factor")
        nc.vector.tensor_scalar(factor[:], old_listed[:], inv_sum[:], None, ALU.mult)
        nc.vector.tensor_tensor(placed[:].indirect(idx4[:]), p[:], factor[:], ALU.mult)

        result = keep.tile([P, T], F32, name="result")
        lo = 0
        for c, width in enumerate(OUT_CHUNKS):
            cols = slice(lo, lo + width)
            nc.vector.tensor_tensor(result[:, cols], placed[:, cols], base_sb[:, cols], ALU.add)
            queue = nc.sync if c % 2 == 0 else nc.scalar
            queue.dma_start(out=out[:, cols], in_=result[:, cols])
            lo = lo + width
